import numpy as np
import ml_dtypes


def mxq(x, axis, fmt="e4m3"):
    dtype, down = {"e4m3": (ml_dtypes.float8_e4m3fn, 7), "e5m2": (ml_dtypes.float8_e5m2, 14)}[fmt]
    v = np.moveaxis(np.asarray(x, np.float32).astype(ml_dtypes.bfloat16).astype(np.float64), axis, -1)
    blocks = v.reshape(v.shape[:-1] + (-1, 32))
    amax = np.abs(blocks).max(-1, keepdims=True)
    byte = np.maximum(np.where(amax > 0, np.frexp(amax)[1] - 1 + 127, 0) - down, 1)
    scale = np.exp2(byte - 127.0)
    codes = (blocks / scale).astype(np.float32).astype(dtype).astype(np.float64)
    return np.moveaxis((codes * scale).reshape(v.shape), -1, axis)


WIDE = False


def mx_kscale(k):
    if not WIDE:
        return np.ones(k)
    levels = np.array([10, -10, 5, -5, 0])
    if k % 512:
        return np.exp2(np.random.permutation(np.resize(levels, k // 32))).repeat(32)
    a = np.empty((k // 512, 16))
    for p in range(k // 512):
        a[p, :8] = np.random.permutation(np.resize(levels, 8))
        for g in range(8):
            far = levels[np.abs(levels - a[p, g]) >= 10]
            a[p, g + 8] = far[np.random.randint(len(far))]
    return np.exp2(a.ravel()).repeat(32)


def f64(x):
    return np.asarray(x).astype(np.float64)


def striped(idx):
    return np.tile(idx.reshape(-1, 16).T, (8, 1)).astype(np.uint16)


def unstriped(offs):
    return offs[:16].T.reshape(-1).astype(np.int64)


def pack_weight(w):
    k, n = w.shape
    w = f64(np.asarray(w, np.float32).astype(ml_dtypes.bfloat16)).reshape(k // 32, 32, n)
    amax = np.abs(w).max(1)
    byte = np.clip(np.where(amax > 0, np.frexp(amax)[1] - 1 + 127 - 7, 1), 1, 254)
    scaled = (w * np.exp2(127.0 - byte)[:, None, :]).reshape(k, n).astype(np.float32)
    words = np.ascontiguousarray(scaled.reshape(k // 512, 128, 4, n).transpose(0, 1, 3, 2)).astype(ml_dtypes.float8_e4m3fn).view(np.uint8)
    return words, np.ascontiguousarray(byte.astype(np.uint8).reshape(k // 512, 16, n))


def unpack_weight(words, scales):
    g, p, n, _ = words.shape
    vals = np.ascontiguousarray(words).view(ml_dtypes.float8_e4m3fn).astype(np.float64) * np.repeat(np.exp2(scales.astype(np.float64) - 127.0), 8, axis=1)[..., None]
    return vals.transpose(0, 1, 3, 2).reshape(g * 512, n)


def silu(v):
    return v / (1.0 + np.exp(-np.maximum(v, -700.0)))


K, T, D, S, V, N = 512, 1024, 4, 512, 256, 128


def setup_inputs():
    n = np.random.standard_normal
    s = mx_kscale(K)[:, None]
    words, scales = pack_weight(n((K, N)) / np.sqrt(K) / s)
    return {
        "xT": (n((K, T)) * s).astype(np.float32),
        "w_words": words,
        "w_scales": scales,
        "b": (0.3 * n((N, 1))).astype(np.float32),
        "gate": np.tile(np.random.uniform(0.2, 1.0, (D, 1, V)) / np.sqrt(D), (1, N, 1)).astype(np.float32),
        "offs": striped(np.random.permutation(T)[:S]),
        "pos1": striped(np.random.permutation(S)[:V]),
        "pos2": striped(np.random.permutation(S)[:V]),
        "pos3": striped(np.random.permutation(S)[:V]),
        "pos4": striped(np.random.permutation(S)[:V]),
    }


def reference(xT, w_words, w_scales, b, gate, offs, pos1, pos2, pos3, pos4):
    w = unpack_weight(w_words, w_scales)
    idx = unstriped(offs)
    xq = mxq(f64(xT)[:, idx], 0, "e4m3")
    y = w.T @ xq
    y = silu(y + f64(b))
    return sum(f64(gate[d]) * y[:, unstriped(p)] for d, p in enumerate((pos1, pos2, pos3, pos4)))

@@ -1,0 +1,119 @@
+from contextlib import ExitStack
+
+import concourse.mybir as mybir
+
+K, T, D, S, V, N = 512, 1024, 4, 512, 256, 128
+P = 128
+PACK = 4
+PIECE = 256
+LINE = 16
+HALF = V // 2
+
+FLOPS = 2 * K * S * N
+
+F32 = mybir.dt.float32
+BF16 = mybir.dt.bfloat16
+I32 = mybir.dt.int32
+U32 = mybir.dt.uint32
+U16 = mybir.dt.uint16
+U8 = mybir.dt.uint8
+FP8X4 = mybir.dt.float8_e4m3fn_x4
+SILU = mybir.ActivationFunctionType.Silu
+MULT = mybir.AluOpType.mult
+ADD = mybir.AluOpType.add
+
+
+def tile_picked_sub_lin_silu_sub_e_kernel(tc, xT, w_words, w_scales, b, gate, offs, pos1, pos2, pos3, pos4, out):
+    nc = tc.nc
+    with ExitStack() as ctx:
+        keep = ctx.enter_context(tc.tile_pool(name="keep", bufs=1))
+        psum = ctx.enter_context(tc.psum_pool(name="psum", bufs=1))
+
+        offsets = keep.tile([P, S // LINE], U16, name="offsets")
+        places = [keep.tile([P, V // LINE], U16, name=f"places{d}") for d in range(D)]
+        x_rows = [keep.tile([P, T], F32, name=f"x_rows{t}", align_bytes=64) for t in range(PACK)]
+        w_codes = keep.tile([P, N], U32, name="w_codes", align_bytes=64)
+        w_planes = keep.tile([P, N], U8, name="w_planes", align_bytes=64)
+        bias = keep.tile([P, 1], F32, name="bias")
+        gates = keep.tile([P, D, V], F32, name="gates", align_bytes=64)
+        warm = keep.tile([P, 1], F32, name="warm")
+        warm_out = keep.tile([P, 1], F32, name="warm_out")
+
+        nc.gpsimd.memset(warm[:], 0.0)
+        nc.gpsimd.memset(w_planes[:].bitcast(I32), 0)
+        nc.scalar.activation(warm_out[:], warm[:], SILU)
+
+        x_view = xT.rearrange("(p t) c -> p t c", t=PACK)
+        nc.sync.dma_start(offsets[:], offs)
+        for t in range(PACK):
+            nc.sync.dma_start(x_rows[t][:], x_view[:, t, :])
+        nc.sync.dma_start(w_codes[:].bitcast(I32), w_words[0].rearrange("p m r -> p (m r)").bitcast(I32))
+        for q in range(4):
+            nc.sync.dma_start(w_planes[32 * q : 32 * q + 4, :].bitcast(I32), w_scales[0, 4 * q : 4 * q + 4, :].bitcast(I32))
+        nc.sync.dma_start(bias[:], b)
+        for d, pos in enumerate((pos1, pos2, pos3, pos4)):
+            nc.sync.dma_start(places[d][:], pos)
+        nc.sync.dma_start(gates[:], gate.rearrange("d m v -> m d v"))
+
+        picked = keep.tile([P, PACK, S], F32, name="picked", align_bytes=64)
+        grouped = [keep.tile([P, PIECE, PACK], BF16, name=f"grouped{i}", align_bytes=64) for i in range(2)]
+        codes = [keep.tile([P, PIECE], U32, name=f"codes{i}", align_bytes=64) for i in range(2)]
+        planes = [keep.tile([P, PIECE], U8, name=f"planes{i}", align_bytes=64) for i in range(2)]
+        sums = [psum.tile([N, PIECE], F32, name=f"sums{i}") for i in range(2)]
+        y = keep.tile([N, S], F32, name="y", align_bytes=64)
+
+        def cols(i):
+            return slice(i * PIECE, (i + 1) * PIECE)
+
+        def pair(i, t):
+            source = picked[:, t : t + 2, cols(i)].rearrange("p t c -> p c t")
+            return grouped[i][:, :, t : t + 2], source
+
+        for t in range(PACK - 1):
+            nc.vector.tensor_copy(picked[:, t, :], x_rows[t][:].indirect(offsets[:]))
+            if t == 1:
+                for i in range(2):
+                    nc.scalar.copy(*pair(i, 0))
+        for i in range(2):
+            lines = slice(i * PIECE // LINE, (i + 1) * PIECE // LINE)
+            nc.vector.tensor_copy(picked[:, PACK - 1, cols(i)], x_rows[PACK - 1][:].indirect(offsets[:, lines]))
+        nc.scalar.copy(*pair(0, 2))
+        nc.vector.tensor_copy(*pair(1, 2))
+
+        for i in range(2):
+            nc.vector.quantize_mx(
+                out=codes[i][:].bitcast(FP8X4), scales=planes[i][:], in_=grouped[i][:].rearrange("p c t -> p (c t)")
+            )
+            nc.tensor.matmul_mx(
+                out=sums[i][:],
+                lhsT=w_codes[:].bitcast(FP8X4),
+                lhsT_scale=w_planes[:],
+                rhs=codes[i][:].bitcast(FP8X4),
+                rhs_scale=planes[i][:],
+                start=True,
+                stop=True,
+            )
+            nc.scalar.activation(y[:, cols(i)], sums[i][:], SILU, bias=bias[:])
+
+        terms = [keep.tile([N, V], F32, name=f"term{d}", align_bytes=64) for d in range(D - 1)]
+        last = [keep.tile([N, HALF], F32, name=f"last{h}", align_bytes=64) for h in range(2)]
+        first_two = keep.tile([N, V], F32, name="first_two", align_bytes=64)
+        first_three = keep.tile([N, V], F32, name="first_three", align_bytes=64)
+        result = [keep.tile([N, HALF], F32, name=f"result{h}", align_bytes=64) for h in range(2)]
+
+        def half(h):
+            return slice(h * HALF, (h + 1) * HALF)
+
+        def last_term(h):
+            lines = slice(h * HALF // LINE, (h + 1) * HALF // LINE)
+            nc.vector.tensor_tensor(last[h][:], y[:].indirect(places[D - 1][:, lines]), gates[:, D - 1, half(h)], MULT)
+
+        for d in range(D - 1):
+            nc.vector.tensor_tensor(terms[d][:], y[:].indirect(places[d][:]), gates[:, d, :], MULT)
+        nc.vector.tensor_tensor(first_two[:], terms[0][:], terms[1][:], ADD)
+        last_term(0)
+        nc.vector.tensor_tensor(first_three[:], first_two[:], terms[2][:], ADD)
+        last_term(1)
+        for h in range(2):
+            nc.vector.tensor_tensor(result[h][:], first_three[:, half(h)], last[h][:], ADD)
+            nc.sync.dma_start(out[:, half(h)], result[h][:])

@@ -5,7 +5,7 @@ import concourse.mybir as mybir
 K, T, D, S, V, N = 512, 1024, 4, 512, 256, 128
 P = 128
 PACK = 4
-PIECE = 256
+PIECES = ((0, 256), (256, 384), (384, 512))
 LINE = 16
 HALF = V // 2
 
@@ -39,7 +39,7 @@ def tile_picked_sub_lin_silu_sub_e_kernel(tc, xT, w_words, w_scales, b, gate, of
         warm = keep.tile([P, 1], F32, name="warm")
         warm_out = keep.tile([P, 1], F32, name="warm_out")
 
-        nc.gpsimd.memset(warm[:], 0.0)
+        nc.vector.memset(warm[:], 0.0)
         nc.gpsimd.memset(w_planes[:].bitcast(I32), 0)
         nc.scalar.activation(warm_out[:], warm[:], SILU)
 
@@ -47,23 +47,24 @@ def tile_picked_sub_lin_silu_sub_e_kernel(tc, xT, w_words, w_scales, b, gate, of
         nc.sync.dma_start(offsets[:], offs)
         for t in range(PACK):
             nc.sync.dma_start(x_rows[t][:], x_view[:, t, :])
-        nc.sync.dma_start(w_codes[:].bitcast(I32), w_words[0].rearrange("p m r -> p (m r)").bitcast(I32))
         for q in range(4):
-            nc.sync.dma_start(w_planes[32 * q : 32 * q + 4, :].bitcast(I32), w_scales[0, 4 * q : 4 * q + 4, :].bitcast(I32))
+            nc.gpsimd.dma_start(w_planes[32 * q : 32 * q + 4, :].bitcast(I32), w_scales[0, 4 * q : 4 * q + 4, :].bitcast(I32))
+        nc.sync.dma_start(w_codes[:].bitcast(I32), w_words[0].rearrange("p m r -> p (m r)").bitcast(I32))
         nc.sync.dma_start(bias[:], b)
+        nc.sync.dma_start(gates[:], gate.rearrange("d m v -> m d v"))
         for d, pos in enumerate((pos1, pos2, pos3, pos4)):
             nc.sync.dma_start(places[d][:], pos)
-        nc.sync.dma_start(gates[:], gate.rearrange("d m v -> m d v"))
 
         picked = keep.tile([P, PACK, S], F32, name="picked", align_bytes=64)
-        grouped = [keep.tile([P, PIECE, PACK], BF16, name=f"grouped{i}", align_bytes=64) for i in range(2)]
-        codes = [keep.tile([P, PIECE], U32, name=f"codes{i}", align_bytes=64) for i in range(2)]
-        planes = [keep.tile([P, PIECE], U8, name=f"planes{i}", align_bytes=64) for i in range(2)]
-        sums = [psum.tile([N, PIECE], F32, name=f"sums{i}") for i in range(2)]
+        widths = [end - start for start, end in PIECES]
+        grouped = [keep.tile([P, n, PACK], BF16, name=f"grouped{i}", align_bytes=64) for i, n in enumerate(widths)]
+        codes = [keep.tile([P, n], U32, name=f"codes{i}", align_bytes=64) for i, n in enumerate(widths)]
+        planes = [keep.tile([P, n], U8, name=f"planes{i}", align_bytes=64) for i, n in enumerate(widths)]
+        sums = [psum.tile([N, n], F32, name=f"sums{i}") for i, n in enumerate(widths)]
         y = keep.tile([N, S], F32, name="y", align_bytes=64)
 
         def cols(i):
-            return slice(i * PIECE, (i + 1) * PIECE)
+            return slice(*PIECES[i])
 
         def pair(i, t):
             source = picked[:, t : t + 2, cols(i)].rearrange("p t c -> p c t")
@@ -72,15 +73,16 @@ def tile_picked_sub_lin_silu_sub_e_kernel(tc, xT, w_words, w_scales, b, gate, of
         for t in range(PACK - 1):
             nc.vector.tensor_copy(picked[:, t, :], x_rows[t][:].indirect(offsets[:]))
             if t == 1:
-                for i in range(2):
+                for i in range(3):
                     nc.scalar.copy(*pair(i, 0))
-        for i in range(2):
-            lines = slice(i * PIECE // LINE, (i + 1) * PIECE // LINE)
+        for i, (start, end) in enumerate(PIECES):
+            lines = slice(start // LINE, end // LINE)
             nc.vector.tensor_copy(picked[:, PACK - 1, cols(i)], x_rows[PACK - 1][:].indirect(offsets[:, lines]))
         nc.scalar.copy(*pair(0, 2))
+        nc.scalar.copy(*pair(2, 2))
         nc.vector.tensor_copy(*pair(1, 2))
 
-        for i in range(2):
+        for i in range(3):
             nc.vector.quantize_mx(
                 out=codes[i][:].bitcast(FP8X4), scales=planes[i][:], in_=grouped[i][:].rearrange("p c t -> p (c t)")
             )

@@ -41,12 +41,12 @@ def tile_picked_sub_lin_silu_sub_e_kernel(tc, xT, w_words, w_scales, b, gate, of
 
         nc.vector.memset(warm[:], 0.0)
         nc.gpsimd.memset(w_planes[:].bitcast(I32), 0)
-        nc.scalar.activation(warm_out[:], warm[:], SILU)
-
         x_view = xT.rearrange("(p t) c -> p t c", t=PACK)
+        nc.scalar.dma_start(x_rows[0][:], x_view[:, 0, :])
         nc.sync.dma_start(offsets[:], offs)
-        for t in range(PACK):
+        for t in range(1, PACK):
             nc.sync.dma_start(x_rows[t][:], x_view[:, t, :])
+        nc.scalar.activation(warm_out[:], warm[:], SILU)
         for q in range(4):
             nc.gpsimd.dma_start(w_planes[32 * q : 32 * q + 4, :].bitcast(I32), w_scales[0, 4 * q : 4 * q + 4, :].bitcast(I32))
         nc.sync.dma_start(w_codes[:].bitcast(I32), w_words[0].rearrange("p m r -> p (m r)").bitcast(I32))
@@ -118,4 +118,4 @@ def tile_picked_sub_lin_silu_sub_e_kernel(tc, xT, w_words, w_scales, b, gate, of
         last_term(1)
         for h in range(2):
             nc.vector.tensor_tensor(result[h][:], first_three[:, half(h)], last[h][:], ADD)
-            nc.sync.dma_start(out[:, half(h)], result[h][:])
+            (nc.scalar, nc.sync)[h].dma_start(out[:, half(h)], result[h][:])

@@ -48,7 +48,7 @@ def tile_picked_sub_lin_silu_sub_e_kernel(tc, xT, w_words, w_scales, b, gate, of
             nc.sync.dma_start(x_rows[t][:], x_view[:, t, :])
         nc.scalar.activation(warm_out[:], warm[:], SILU)
         for q in range(4):
-            nc.gpsimd.dma_start(w_planes[32 * q : 32 * q + 4, :].bitcast(I32), w_scales[0, 4 * q : 4 * q + 4, :].bitcast(I32))
+            (nc.gpsimd if q % 2 else nc.scalar).dma_start(w_planes[32 * q : 32 * q + 4, :].bitcast(I32), w_scales[0, 4 * q : 4 * q + 4, :].bitcast(I32))
         nc.sync.dma_start(w_codes[:].bitcast(I32), w_words[0].rearrange("p m r -> p (m r)").bitcast(I32))
         nc.sync.dma_start(bias[:], b)
         nc.sync.dma_start(gates[:], gate.rearrange("d m v -> m d v"))

from contextlib import ExitStack

import concourse.mybir as mybir

K, T, D, S, V, N = 512, 1024, 4, 512, 256, 128
P = 128
PACK = 4
PIECES = ((0, 256), (256, 384), (384, 512))
LINE = 16
HALF = V // 2

FLOPS = 2 * K * S * N

F32 = mybir.dt.float32
BF16 = mybir.dt.bfloat16
I32 = mybir.dt.int32
U32 = mybir.dt.uint32
U16 = mybir.dt.uint16
U8 = mybir.dt.uint8
FP8X4 = mybir.dt.float8_e4m3fn_x4
SILU = mybir.ActivationFunctionType.Silu
MULT = mybir.AluOpType.mult
ADD = mybir.AluOpType.add


def tile_picked_sub_lin_silu_sub_e_kernel(tc, xT, w_words, w_scales, b, gate, offs, pos1, pos2, pos3, pos4, out):
    nc = tc.nc
    with ExitStack() as ctx:
        keep = ctx.enter_context(tc.tile_pool(name="keep", bufs=1))
        psum = ctx.enter_context(tc.psum_pool(name="psum", bufs=1))

        offsets = keep.tile([P, S // LINE], U16, name="offsets")
        places = [keep.tile([P, V // LINE], U16, name=f"places{d}") for d in range(D)]
        x_rows = [keep.tile([P, T], F32, name=f"x_rows{t}", align_bytes=64) for t in range(PACK)]
        w_codes = keep.tile([P, N], U32, name="w_codes", align_bytes=64)
        w_planes = keep.tile([P, N], U8, name="w_planes", align_bytes=64)
        bias = keep.tile([P, 1], F32, name="bias")
        gates = keep.tile([P, D, V], F32, name="gates", align_bytes=64)
        warm = keep.tile([P, 1], F32, name="warm")
        warm_out = keep.tile([P, 1], F32, name="warm_out")

        nc.vector.memset(warm[:], 0.0)
        nc.gpsimd.memset(w_planes[:].bitcast(I32), 0)
        x_view = xT.rearrange("(p t) c -> p t c", t=PACK)
        nc.scalar.dma_start(x_rows[0][:], x_view[:, 0, :])
        nc.sync.dma_start(offsets[:], offs)
        for t in range(1, PACK):
            nc.sync.dma_start(x_rows[t][:], x_view[:, t, :])
        nc.scalar.activation(warm_out[:], warm[:], SILU)
        for q in range(4):
            (nc.gpsimd if q % 2 else nc.scalar).dma_start(w_planes[32 * q : 32 * q + 4, :].bitcast(I32), w_scales[0, 4 * q : 4 * q + 4, :].bitcast(I32))
        nc.sync.dma_start(w_codes[:].bitcast(I32), w_words[0].rearrange("p m r -> p (m r)").bitcast(I32))
        nc.sync.dma_start(bias[:], b)
        nc.sync.dma_start(gates[:], gate.rearrange("d m v -> m d v"))
        for d, pos in enumerate((pos1, pos2, pos3, pos4)):
            nc.sync.dma_start(places[d][:], pos)

        picked = keep.tile([P, PACK, S], F32, name="picked", align_bytes=64)
        widths = [end - start for start, end in PIECES]
        grouped = [keep.tile([P, n, PACK], BF16, name=f"grouped{i}", align_bytes=64) for i, n in enumerate(widths)]
        codes = [keep.tile([P, n], U32, name=f"codes{i}", align_bytes=64) for i, n in enumerate(widths)]
        planes = [keep.tile([P, n], U8, name=f"planes{i}", align_bytes=64) for i, n in enumerate(widths)]
        sums = [psum.tile([N, n], F32, name=f"sums{i}") for i, n in enumerate(widths)]
        y = keep.tile([N, S], F32, name="y", align_bytes=64)

        def cols(i):
            return slice(*PIECES[i])

        def pair(i, t):
            source = picked[:, t : t + 2, cols(i)].rearrange("p t c -> p c t")
            return grouped[i][:, :, t : t + 2], source

        for t in range(PACK - 1):
            nc.vector.tensor_copy(picked[:, t, :], x_rows[t][:].indirect(offsets[:]))
            if t == 1:
                for i in range(3):
                    nc.scalar.copy(*pair(i, 0))
        for i, (start, end) in enumerate(PIECES):
            lines = slice(start // LINE, end // LINE)
            nc.vector.tensor_copy(picked[:, PACK - 1, cols(i)], x_rows[PACK - 1][:].indirect(offsets[:, lines]))
        nc.scalar.copy(*pair(0, 2))
        nc.scalar.copy(*pair(2, 2))
        nc.vector.tensor_copy(*pair(1, 2))

        for i in range(3):
            nc.vector.quantize_mx(
                out=codes[i][:].bitcast(FP8X4), scales=planes[i][:], in_=grouped[i][:].rearrange("p c t -> p (c t)")
            )
            nc.tensor.matmul_mx(
                out=sums[i][:],
                lhsT=w_codes[:].bitcast(FP8X4),
                lhsT_scale=w_planes[:],
                rhs=codes[i][:].bitcast(FP8X4),
                rhs_scale=planes[i][:],
                start=True,
                stop=True,
            )
            nc.scalar.activation(y[:, cols(i)], sums[i][:], SILU, bias=bias[:])

        terms = [keep.tile([N, V], F32, name=f"term{d}", align_bytes=64) for d in range(D - 1)]
        last = [keep.tile([N, HALF], F32, name=f"last{h}", align_bytes=64) for h in range(2)]
        first_two = keep.tile([N, V], F32, name="first_two", align_bytes=64)
        first_three = keep.tile([N, V], F32, name="first_three", align_bytes=64)
        result = [keep.tile([N, HALF], F32, name=f"result{h}", align_bytes=64) for h in range(2)]

        def half(h):
            return slice(h * HALF, (h + 1) * HALF)

        def last_term(h):
            lines = slice(h * HALF // LINE, (h + 1) * HALF // LINE)
            nc.vector.tensor_tensor(last[h][:], y[:].indirect(places[D - 1][:, lines]), gates[:, D - 1, half(h)], MULT)

        for d in range(D - 1):
            nc.vector.tensor_tensor(terms[d][:], y[:].indirect(places[d][:]), gates[:, d, :], MULT)
        nc.vector.tensor_tensor(first_two[:], terms[0][:], terms[1][:], ADD)
        last_term(0)
        nc.vector.tensor_tensor(first_three[:], first_two[:], terms[2][:], ADD)
        last_term(1)
        for h in range(2):
            nc.vector.tensor_tensor(result[h][:], first_three[:, half(h)], last[h][:], ADD)
            (nc.scalar, nc.sync)[h].dma_start(out[:, half(h)], result[h][:])
